import numpy as np
import ml_dtypes

BF16 = ml_dtypes.bfloat16


def bf(x):
    return np.asarray(x, np.float32).astype(BF16)


def f32(x):
    return np.asarray(x, np.float32)


def f64(x):
    return np.asarray(x).astype(np.float64)


def striped(idx):
    return np.concatenate([l.reshape(-1, 16).T for l in idx])


def rows(idx, k):
    return np.tile(np.repeat(idx, 16, axis=0), (k // (16 * 8), 1))


def look(tab, idx):
    return np.take_along_axis(f64(tab), rows(idx, len(tab)), axis=1)


K, S, V, N = 128, 2048, 1024, 1024


def setup_inputs():
    return {"tab": f32(np.random.standard_normal((2, K, S))), "offs": striped(np.stack([np.random.permutation(S)[:N] for _ in range(8)]))}


def reference(tab, offs):
    idx = np.stack([g.T.reshape(-1) for g in np.split(offs, 8)])
    x = ((look(tab[0], idx) - 0.125) * 1.5) * (np.tanh(look(tab[1], idx)))
    return x

@@ -1,0 +1,37 @@
+import concourse.mybir as mybir
+
+F32 = mybir.dt.float32
+U16 = mybir.dt.uint16
+ALU = mybir.AluOpType
+TANH = mybir.ActivationFunctionType.Tanh
+
+SHIFT = 0.125
+SCALE = 1.5
+GROUP = 16
+PIECE = 512
+
+
+def tile_lookup_vg_nrmtanh_out_kernel(tc, tab, offs, out):
+    nc = tc.nc
+    rows, places = tab.shape[1], tab.shape[2]
+    entries = out.shape[1]
+
+    with tc.tile_pool(name="held", bufs=1) as held:
+        offsets = held.tile([rows, entries // GROUP], U16, name="offsets")
+        values = held.tile([rows, places], F32, name="values")
+        gates = held.tile([rows, places], F32, name="gates")
+        nc.sync.dma_start(offsets[:], offs)
+        nc.sync.dma_start(values[:], tab[0])
+        nc.sync.dma_start(gates[:], tab[1])
+
+        for piece in range(entries // PIECE):
+            piece_offsets = offsets[:, piece * PIECE // GROUP : (piece + 1) * PIECE // GROUP]
+            scaled = held.tile([rows, PIECE], F32, name=f"scaled{piece}")
+            gate = held.tile([rows, PIECE], F32, name=f"gate{piece}")
+            product = held.tile([rows, PIECE], F32, name=f"product{piece}")
+            nc.vector.tensor_scalar(
+                scaled[:], values[:].indirect(piece_offsets), SHIFT, SCALE, ALU.subtract, ALU.mult
+            )
+            nc.scalar.activation(gate[:], gates[:].indirect(piece_offsets), TANH)
+            nc.vector.tensor_tensor(product[:], scaled[:], gate[:], ALU.mult)
+            nc.sync.dma_start(out[:, piece * PIECE : (piece + 1) * PIECE], product[:])

@@ -20,9 +20,14 @@ def tile_lookup_vg_nrmtanh_out_kernel(tc, tab, offs, out):
         offsets = held.tile([rows, entries // GROUP], U16, name="offsets")
         values = held.tile([rows, places], F32, name="values")
         gates = held.tile([rows, places], F32, name="gates")
-        nc.sync.dma_start(offsets[:], offs)
         nc.sync.dma_start(values[:], tab[0])
+        nc.sync.dma_start(offsets[:], offs)
         nc.sync.dma_start(gates[:], tab[1])
+
+        warm_in = held.tile([rows, 1], F32, name="warm_in")
+        warm_out = held.tile([rows, 1], F32, name="warm_out")
+        nc.vector.memset(warm_in[:], 0.0)
+        nc.scalar.activation(warm_out[:], warm_in[:], TANH)
 
         for piece in range(entries // PIECE):
             piece_offsets = offsets[:, piece * PIECE // GROUP : (piece + 1) * PIECE // GROUP]

@@ -9,6 +9,7 @@ SHIFT = 0.125
 SCALE = 1.5
 GROUP = 16
 PIECE = 512
+STORE = 256
 
 
 def tile_lookup_vg_nrmtanh_out_kernel(tc, tab, offs, out):
@@ -33,10 +34,14 @@ def tile_lookup_vg_nrmtanh_out_kernel(tc, tab, offs, out):
             piece_offsets = offsets[:, piece * PIECE // GROUP : (piece + 1) * PIECE // GROUP]
             scaled = held.tile([rows, PIECE], F32, name=f"scaled{piece}")
             gate = held.tile([rows, PIECE], F32, name=f"gate{piece}")
-            product = held.tile([rows, PIECE], F32, name=f"product{piece}")
             nc.vector.tensor_scalar(
                 scaled[:], values[:].indirect(piece_offsets), SHIFT, SCALE, ALU.subtract, ALU.mult
             )
             nc.scalar.activation(gate[:], gates[:].indirect(piece_offsets), TANH)
-            nc.vector.tensor_tensor(product[:], scaled[:], gate[:], ALU.mult)
-            nc.sync.dma_start(out[:, piece * PIECE : (piece + 1) * PIECE], product[:])
+            for start in range(0, PIECE, STORE):
+                column = piece * PIECE + start
+                product = held.tile([rows, STORE], F32, name=f"product{column}")
+                nc.vector.tensor_tensor(
+                    product[:], scaled[:, start : start + STORE], gate[:, start : start + STORE], ALU.mult
+                )
+                nc.sync.dma_start(out[:, column : column + STORE], product[:])

@@ -25,11 +25,6 @@ def tile_lookup_vg_nrmtanh_out_kernel(tc, tab, offs, out):
         nc.sync.dma_start(offsets[:], offs)
         nc.sync.dma_start(gates[:], tab[1])
 
-        warm_in = held.tile([rows, 1], F32, name="warm_in")
-        warm_out = held.tile([rows, 1], F32, name="warm_out")
-        nc.vector.memset(warm_in[:], 0.0)
-        nc.scalar.activation(warm_out[:], warm_in[:], TANH)
-
         for piece in range(entries // PIECE):
             piece_offsets = offsets[:, piece * PIECE // GROUP : (piece + 1) * PIECE // GROUP]
             scaled = held.tile([rows, PIECE], F32, name=f"scaled{piece}")

@@ -10,6 +10,7 @@ SCALE = 1.5
 GROUP = 16
 PIECE = 512
 STORE = 256
+BURST = 256
 
 
 def tile_lookup_vg_nrmtanh_out_kernel(tc, tab, offs, out):
@@ -19,23 +20,28 @@ def tile_lookup_vg_nrmtanh_out_kernel(tc, tab, offs, out):
 
     with tc.tile_pool(name="held", bufs=1) as held:
         offsets = held.tile([rows, entries // GROUP], U16, name="offsets")
-        values = held.tile([rows, places], F32, name="values")
-        gates = held.tile([rows, places], F32, name="gates")
+        values = held.tile([rows, places], F32, name="values", align_bytes=BURST)
+        gates = held.tile([rows, places], F32, name="gates", align_bytes=BURST)
         nc.sync.dma_start(values[:], tab[0])
         nc.sync.dma_start(offsets[:], offs)
         nc.sync.dma_start(gates[:], tab[1])
+
+        scale = held.tile([rows, 1], F32, name="scale")
+        bias = held.tile([rows, 1], F32, name="bias")
+        nc.vector.memset(scale[:], SCALE)
+        nc.scalar.mul(bias[:], scale[:], -SHIFT)
 
         for piece in range(entries // PIECE):
             piece_offsets = offsets[:, piece * PIECE // GROUP : (piece + 1) * PIECE // GROUP]
             scaled = held.tile([rows, PIECE], F32, name=f"scaled{piece}")
             gate = held.tile([rows, PIECE], F32, name=f"gate{piece}")
             nc.vector.tensor_scalar(
-                scaled[:], values[:].indirect(piece_offsets), SHIFT, SCALE, ALU.subtract, ALU.mult
+                scaled[:], values[:].indirect(piece_offsets), scale[:], bias[:], ALU.mult, ALU.add
             )
             nc.scalar.activation(gate[:], gates[:].indirect(piece_offsets), TANH)
             for start in range(0, PIECE, STORE):
                 column = piece * PIECE + start
-                product = held.tile([rows, STORE], F32, name=f"product{column}")
+                product = held.tile([rows, STORE], F32, name=f"product{column}", align_bytes=BURST)
                 nc.vector.tensor_tensor(
                     product[:], scaled[:, start : start + STORE], gate[:, start : start + STORE], ALU.mult
                 )

@@ -9,7 +9,7 @@ SHIFT = 0.125
 SCALE = 1.5
 GROUP = 16
 PIECE = 512
-STORE = 256
+LEAD = 192
 BURST = 256
 
 
@@ -39,10 +39,9 @@ def tile_lookup_vg_nrmtanh_out_kernel(tc, tab, offs, out):
                 scaled[:], values[:].indirect(piece_offsets), scale[:], bias[:], ALU.mult, ALU.add
             )
             nc.scalar.activation(gate[:], gates[:].indirect(piece_offsets), TANH)
-            for start in range(0, PIECE, STORE):
+            cuts = (0, PIECE) if piece == 0 else (0, LEAD, PIECE)
+            for start, stop in zip(cuts, cuts[1:]):
                 column = piece * PIECE + start
-                product = held.tile([rows, STORE], F32, name=f"product{column}", align_bytes=BURST)
-                nc.vector.tensor_tensor(
-                    product[:], scaled[:, start : start + STORE], gate[:, start : start + STORE], ALU.mult
-                )
-                nc.sync.dma_start(out[:, column : column + STORE], product[:])
+                product = held.tile([rows, stop - start], F32, name=f"product{column}", align_bytes=BURST)
+                nc.vector.tensor_tensor(product[:], scaled[:, start:stop], gate[:, start:stop], ALU.mult)
+                nc.sync.dma_start(out[:, column : column + stop - start], product[:])

@@ -31,17 +31,20 @@ def tile_lookup_vg_nrmtanh_out_kernel(tc, tab, offs, out):
         nc.vector.memset(scale[:], SCALE)
         nc.scalar.mul(bias[:], scale[:], -SHIFT)
 
-        for piece in range(entries // PIECE):
-            piece_offsets = offsets[:, piece * PIECE // GROUP : (piece + 1) * PIECE // GROUP]
-            scaled = held.tile([rows, PIECE], F32, name=f"scaled{piece}")
-            gate = held.tile([rows, PIECE], F32, name=f"gate{piece}")
+        pieces = range(entries // PIECE)
+        lists = [offsets[:, piece * PIECE // GROUP : (piece + 1) * PIECE // GROUP] for piece in pieces]
+        scaled = [held.tile([rows, PIECE], F32, name=f"scaled{piece}") for piece in pieces]
+        for piece in reversed(pieces):
             nc.vector.tensor_scalar(
-                scaled[:], values[:].indirect(piece_offsets), scale[:], bias[:], ALU.mult, ALU.add
+                scaled[piece][:], values[:].indirect(lists[piece]), scale[:], bias[:], ALU.mult, ALU.add
             )
-            nc.scalar.activation(gate[:], gates[:].indirect(piece_offsets), TANH)
+
+        for piece in pieces:
+            gate = held.tile([rows, PIECE], F32, name=f"gate{piece}")
+            nc.scalar.activation(gate[:], gates[:].indirect(lists[piece]), TANH)
             cuts = (0, PIECE) if piece == 0 else (0, LEAD, PIECE)
             for start, stop in zip(cuts, cuts[1:]):
                 column = piece * PIECE + start
                 product = held.tile([rows, stop - start], F32, name=f"product{column}", align_bytes=BURST)
-                nc.vector.tensor_tensor(product[:], scaled[:, start:stop], gate[:, start:stop], ALU.mult)
+                nc.vector.tensor_tensor(product[:], scaled[piece][:, start:stop], gate[:, start:stop], ALU.mult)
                 nc.sync.dma_start(out[:, column : column + stop - start], product[:])

@@ -22,21 +22,18 @@ def tile_lookup_vg_nrmtanh_out_kernel(tc, tab, offs, out):
         offsets = held.tile([rows, entries // GROUP], U16, name="offsets")
         values = held.tile([rows, places], F32, name="values", align_bytes=BURST)
         gates = held.tile([rows, places], F32, name="gates", align_bytes=BURST)
-        nc.sync.dma_start(values[:], tab[0])
+        half = places // 2
+        nc.sync.dma_start(values[:, :half], tab[0, :, :half])
+        nc.scalar.dma_start(values[:, half:], tab[0, :, half:])
+        nc.scalar.dma_start(gates[:], tab[1])
         nc.sync.dma_start(offsets[:], offs)
-        nc.sync.dma_start(gates[:], tab[1])
-
-        scale = held.tile([rows, 1], F32, name="scale")
-        bias = held.tile([rows, 1], F32, name="bias")
-        nc.vector.memset(scale[:], SCALE)
-        nc.scalar.mul(bias[:], scale[:], -SHIFT)
 
         pieces = range(entries // PIECE)
         lists = [offsets[:, piece * PIECE // GROUP : (piece + 1) * PIECE // GROUP] for piece in pieces]
         scaled = [held.tile([rows, PIECE], F32, name=f"scaled{piece}") for piece in pieces]
         for piece in reversed(pieces):
             nc.vector.tensor_scalar(
-                scaled[piece][:], values[:].indirect(lists[piece]), scale[:], bias[:], ALU.mult, ALU.add
+                scaled[piece][:], values[:].indirect(lists[piece]), SHIFT, SCALE, ALU.subtract, ALU.mult
             )
 
         for piece in pieces:

@@ -39,7 +39,7 @@ def tile_lookup_vg_nrmtanh_out_kernel(tc, tab, offs, out):
         for piece in pieces:
             gate = held.tile([rows, PIECE], F32, name=f"gate{piece}")
             nc.scalar.activation(gate[:], gates[:].indirect(lists[piece]), TANH)
-            cuts = (0, PIECE) if piece == 0 else (0, LEAD, PIECE)
+            cuts = (0, LEAD, PIECE)
             for start, stop in zip(cuts, cuts[1:]):
                 column = piece * PIECE + start
                 product = held.tile([rows, stop - start], F32, name=f"product{column}", align_bytes=BURST)

@@ -10,6 +10,7 @@ SCALE = 1.5
 GROUP = 16
 PIECE = 512
 LEAD = 192
+SHARE = 512
 BURST = 256
 
 
@@ -22,18 +23,22 @@ def tile_lookup_vg_nrmtanh_out_kernel(tc, tab, offs, out):
         offsets = held.tile([rows, entries // GROUP], U16, name="offsets")
         values = held.tile([rows, places], F32, name="values", align_bytes=BURST)
         gates = held.tile([rows, places], F32, name="gates", align_bytes=BURST)
-        half = places // 2
-        nc.sync.dma_start(values[:, :half], tab[0, :, :half])
-        nc.scalar.dma_start(values[:, half:], tab[0, :, half:])
+        nc.sync.dma_start(values[:, SHARE:], tab[0, :, SHARE:])
+        nc.scalar.dma_start(values[:, :SHARE], tab[0, :, :SHARE])
         nc.scalar.dma_start(gates[:], tab[1])
         nc.sync.dma_start(offsets[:], offs)
+
+        scale = held.tile([rows, 1], F32, name="scale")
+        bias = held.tile([rows, 1], F32, name="bias")
+        nc.gpsimd.memset(scale[:], SCALE)
+        nc.scalar.mul(bias[:], scale[:], -SHIFT)
 
         pieces = range(entries // PIECE)
         lists = [offsets[:, piece * PIECE // GROUP : (piece + 1) * PIECE // GROUP] for piece in pieces]
         scaled = [held.tile([rows, PIECE], F32, name=f"scaled{piece}") for piece in pieces]
         for piece in reversed(pieces):
             nc.vector.tensor_scalar(
-                scaled[piece][:], values[:].indirect(lists[piece]), SHIFT, SCALE, ALU.subtract, ALU.mult
+                scaled[piece][:], values[:].indirect(lists[piece]), scale[:], bias[:], ALU.mult, ALU.add
             )
 
         for piece in pieces:

@@ -10,7 +10,6 @@ SCALE = 1.5
 GROUP = 16
 PIECE = 512
 LEAD = 192
-SHARE = 512
 BURST = 256
 
 
@@ -22,16 +21,20 @@ def tile_lookup_vg_nrmtanh_out_kernel(tc, tab, offs, out):
     with tc.tile_pool(name="held", bufs=1) as held:
         offsets = held.tile([rows, entries // GROUP], U16, name="offsets")
         values = held.tile([rows, places], F32, name="values", align_bytes=BURST)
-        gates = held.tile([rows, places], F32, name="gates", align_bytes=BURST)
-        nc.sync.dma_start(values[:, SHARE:], tab[0, :, SHARE:])
-        nc.scalar.dma_start(values[:, :SHARE], tab[0, :, :SHARE])
-        nc.scalar.dma_start(gates[:], tab[1])
-        nc.sync.dma_start(offsets[:], offs)
+        nc.sync.dma_start(values[:], tab[0])
 
         scale = held.tile([rows, 1], F32, name="scale")
+        shift = held.tile([rows, 1], F32, name="shift", tag="gates", align_bytes=BURST)
+        scaled_shift = held.tile([rows, 1], F32, name="scaled_shift")
         bias = held.tile([rows, 1], F32, name="bias")
         nc.gpsimd.memset(scale[:], SCALE)
-        nc.scalar.mul(bias[:], scale[:], -SHIFT)
+        nc.gpsimd.memset(shift[:], SHIFT)
+        nc.vector.tensor_tensor(scaled_shift[:], shift[:], scale[:], ALU.mult)
+
+        gates = held.tile([rows, places], F32, name="gates", tag="gates", align_bytes=BURST)
+        nc.scalar.dma_start(gates[:], tab[1])
+        nc.sync.dma_start(offsets[:], offs)
+        nc.scalar.mul(bias[:], scaled_shift[:], -1.0)
 
         pieces = range(entries // PIECE)
         lists = [offsets[:, piece * PIECE // GROUP : (piece + 1) * PIECE // GROUP] for piece in pieces]

@@ -25,16 +25,14 @@ def tile_lookup_vg_nrmtanh_out_kernel(tc, tab, offs, out):
 
         scale = held.tile([rows, 1], F32, name="scale")
         shift = held.tile([rows, 1], F32, name="shift", tag="gates", align_bytes=BURST)
-        scaled_shift = held.tile([rows, 1], F32, name="scaled_shift")
         bias = held.tile([rows, 1], F32, name="bias")
-        nc.gpsimd.memset(scale[:], SCALE)
         nc.gpsimd.memset(shift[:], SHIFT)
-        nc.vector.tensor_tensor(scaled_shift[:], shift[:], scale[:], ALU.mult)
+        nc.gpsimd.memset(scale[:], SCALE)
+        nc.scalar.mul(bias[:], shift[:], -SCALE)
 
         gates = held.tile([rows, places], F32, name="gates", tag="gates", align_bytes=BURST)
         nc.scalar.dma_start(gates[:], tab[1])
         nc.sync.dma_start(offsets[:], offs)
-        nc.scalar.mul(bias[:], scaled_shift[:], -1.0)
 
         pieces = range(entries // PIECE)
         lists = [offsets[:, piece * PIECE // GROUP : (piece + 1) * PIECE // GROUP] for piece in pieces]

@@ -42,12 +42,16 @@ def tile_lookup_vg_nrmtanh_out_kernel(tc, tab, offs, out):
                 scaled[piece][:], values[:].indirect(lists[piece]), scale[:], bias[:], ALU.mult, ALU.add
             )
 
+        def multiply_and_store(piece, gate, start, stop, queue):
+            column = piece * PIECE + start
+            product = held.tile([rows, stop - start], F32, name=f"product{column}", align_bytes=BURST)
+            nc.vector.tensor_tensor(product[:], scaled[piece][:, start:stop], gate[:, start:stop], ALU.mult)
+            queue.dma_start(out[:, column : column + stop - start], product[:])
+
+        gate = [held.tile([rows, PIECE], F32, name=f"gate{piece}") for piece in pieces]
         for piece in pieces:
-            gate = held.tile([rows, PIECE], F32, name=f"gate{piece}")
-            nc.scalar.activation(gate[:], gates[:].indirect(lists[piece]), TANH)
-            cuts = (0, LEAD, PIECE)
-            for start, stop in zip(cuts, cuts[1:]):
-                column = piece * PIECE + start
-                product = held.tile([rows, stop - start], F32, name=f"product{column}", align_bytes=BURST)
-                nc.vector.tensor_tensor(product[:], scaled[piece][:, start:stop], gate[:, start:stop], ALU.mult)
-                nc.sync.dma_start(out[:, column : column + stop - start], product[:])
+            nc.scalar.activation(gate[piece][:], gates[:].indirect(lists[piece]), TANH)
+
+        multiply_and_store(0, gate[0], 0, PIECE, nc.scalar)
+        multiply_and_store(1, gate[1], 0, LEAD, nc.sync)
+        multiply_and_store(1, gate[1], LEAD, PIECE, nc.sync)

@@ -52,6 +52,6 @@ def tile_lookup_vg_nrmtanh_out_kernel(tc, tab, offs, out):
         for piece in pieces:
             nc.scalar.activation(gate[piece][:], gates[:].indirect(lists[piece]), TANH)
 
-        multiply_and_store(0, gate[0], 0, PIECE, nc.scalar)
-        multiply_and_store(1, gate[1], 0, LEAD, nc.sync)
+        multiply_and_store(0, gate[0], 0, PIECE, nc.sync)
+        multiply_and_store(1, gate[1], 0, LEAD, nc.scalar)
         multiply_and_store(1, gate[1], LEAD, PIECE, nc.sync)

@@ -26,8 +26,8 @@ def tile_lookup_vg_nrmtanh_out_kernel(tc, tab, offs, out):
         scale = held.tile([rows, 1], F32, name="scale")
         shift = held.tile([rows, 1], F32, name="shift", tag="gates", align_bytes=BURST)
         bias = held.tile([rows, 1], F32, name="bias")
-        nc.gpsimd.memset(shift[:], SHIFT)
-        nc.gpsimd.memset(scale[:], SCALE)
+        nc.vector.memset(shift[:], SHIFT)
+        nc.vector.memset(scale[:], SCALE)
         nc.scalar.mul(bias[:], shift[:], -SCALE)
 
         gates = held.tile([rows, places], F32, name="gates", tag="gates", align_bytes=BURST)

@@ -27,7 +27,7 @@ def tile_lookup_vg_nrmtanh_out_kernel(tc, tab, offs, out):
         shift = held.tile([rows, 1], F32, name="shift", tag="gates", align_bytes=BURST)
         bias = held.tile([rows, 1], F32, name="bias")
         nc.vector.memset(shift[:], SHIFT)
-        nc.vector.memset(scale[:], SCALE)
+        nc.scalar.mul(scale[:], shift[:], SCALE / SHIFT)
         nc.scalar.mul(bias[:], shift[:], -SCALE)
 
         gates = held.tile([rows, places], F32, name="gates", tag="gates", align_bytes=BURST)

import concourse.mybir as mybir

F32 = mybir.dt.float32
U16 = mybir.dt.uint16
ALU = mybir.AluOpType
TANH = mybir.ActivationFunctionType.Tanh

SHIFT = 0.125
SCALE = 1.5
GROUP = 16
PIECE = 512
LEAD = 192
BURST = 256


def tile_lookup_vg_nrmtanh_out_kernel(tc, tab, offs, out):
    nc = tc.nc
    rows, places = tab.shape[1], tab.shape[2]
    entries = out.shape[1]

    with tc.tile_pool(name="held", bufs=1) as held:
        offsets = held.tile([rows, entries // GROUP], U16, name="offsets")
        values = held.tile([rows, places], F32, name="values", align_bytes=BURST)
        nc.sync.dma_start(values[:], tab[0])

        scale = held.tile([rows, 1], F32, name="scale")
        shift = held.tile([rows, 1], F32, name="shift", tag="gates", align_bytes=BURST)
        bias = held.tile([rows, 1], F32, name="bias")
        nc.vector.memset(shift[:], SHIFT)
        nc.scalar.mul(scale[:], shift[:], SCALE / SHIFT)
        nc.scalar.mul(bias[:], shift[:], -SCALE)

        gates = held.tile([rows, places], F32, name="gates", tag="gates", align_bytes=BURST)
        nc.scalar.dma_start(gates[:], tab[1])
        nc.sync.dma_start(offsets[:], offs)

        pieces = range(entries // PIECE)
        lists = [offsets[:, piece * PIECE // GROUP : (piece + 1) * PIECE // GROUP] for piece in pieces]
        scaled = [held.tile([rows, PIECE], F32, name=f"scaled{piece}") for piece in pieces]
        for piece in reversed(pieces):
            nc.vector.tensor_scalar(
                scaled[piece][:], values[:].indirect(lists[piece]), scale[:], bias[:], ALU.mult, ALU.add
            )

        def multiply_and_store(piece, gate, start, stop, queue):
            column = piece * PIECE + start
            product = held.tile([rows, stop - start], F32, name=f"product{column}", align_bytes=BURST)
            nc.vector.tensor_tensor(product[:], scaled[piece][:, start:stop], gate[:, start:stop], ALU.mult)
            queue.dma_start(out[:, column : column + stop - start], product[:])

        gate = [held.tile([rows, PIECE], F32, name=f"gate{piece}") for piece in pieces]
        for piece in pieces:
            nc.scalar.activation(gate[piece][:], gates[:].indirect(lists[piece]), TANH)

        multiply_and_store(0, gate[0], 0, PIECE, nc.sync)
        multiply_and_store(1, gate[1], 0, LEAD, nc.scalar)
        multiply_and_store(1, gate[1], LEAD, PIECE, nc.sync)
